import numpy as np, ml_dtypes
CORES = [24,32,56,88,96,104,30,38,62,94,102,110]
N = 12
B, S = 16, 256
CAPP = 4
def entries(a): return a.T.reshape(-1)
def pack(v, P): return np.ascontiguousarray(np.asarray(v, np.int32).reshape(-1, P).T)
def lists(rng, how):
    Q = rng.integers(0, N * B, N * B)
    O = np.stack([rng.permutation(np.repeat(rng.permutation(N)[:B // CAPP], CAPP)) if how == "full" else rng.permutation(np.repeat(np.arange(N), CAPP))[:B] for r in range(N)])
    Q = (B * O + Q.reshape(N, B) % B).reshape(-1)
    if how == "alike": Q = (B * O + rng.integers(B)).reshape(-1)
    if how == "edge": Q = (B * O + np.where(rng.random((N, B)) < 0.5, 0, B - 1)).reshape(-1)
    if how == "full": Q = (B * O + (rng.integers(B) + np.stack([np.array([np.sum(O[r, :i] == O[r, i]) for i in range(B)]) for r in range(N)])) % B).reshape(-1)
    if how == "sorted": Q = np.sort(Q.reshape(N, B), axis=1).reshape(-1)
    return {"parent": np.broadcast_to(pack(Q, 16), (N, 16, N * B // 16)).copy()}
def setup_inputs(rng):
    return dict({"c": rng.standard_normal((N, 128, B * S), dtype=np.float32).astype(ml_dtypes.bfloat16)}, **lists(rng, "uniform"))
def setup_inputs_alike(rng):
    d = setup_inputs(rng); d.update(lists(rng, "alike"))
    for k in ("c",): d[k] = (d[k].astype(np.float32) * 1048576.0).astype(d[k].dtype)
    return d
def setup_inputs_edge(rng):
    d = setup_inputs(rng); d.update(lists(rng, "edge"))
    for k in ("c",): d[k] = (d[k].astype(np.float32) * (1 / 1024.0)).astype(d[k].dtype)
    return d
def setup_inputs_full(rng):
    d = setup_inputs(rng); d.update(lists(rng, "full"))
    return d
def setup_inputs_sorted(rng):
    d = setup_inputs(rng); d.update(lists(rng, "sorted"))
    return d
def check_inputs(x):
    bad = []
    if x["parent"].min() < 0 or x["parent"].max() >= N * B: bad.append("parent out of range")
    if not all(np.array_equal(a, x["parent"][0]) for a in x["parent"]): bad.append("parent isn't alike on all ranks")
    if max(int(np.bincount(q // B, minlength=N).max()) for q in entries(x["parent"][0]).reshape(N, B)) > CAPP: bad.append("more than CAPP beams of a rank have their parents on one rank")
    return bad
def reference(c, parent):
    A = np.concatenate(list(c), axis=1).reshape(128, N * B, S)
    Y = A[:, entries(parent[0]), :]
    return {"y": np.stack([Y[:, B * r:B * r + B].reshape(128, B * S) for r in range(N)])}

import numpy as np
from concourse.bass import DstId, RemoteDMATransfer
from concourse.mybir import dt, AluOpType, AxisListType, ActivationFunctionType

NR, B, S, CAPP = 12, 16, 256, 4
PK = CAPP * S
CW = B * S
WIN = CW + (NR - 1) * PK
OC = PK // 16

SCRATCH = {
    "big": ("sbuf", [128, WIN], "bfloat16"),
    "pk": ("sbuf", [128, NR * PK], "bfloat16"),
    "ysb": ("sbuf", [128, CW], "bfloat16"),
    "offs": ("sbuf", [128, NR * OC], "uint16"),
    "offr": ("sbuf", [128, B * 16], "uint16"),
    "a4": ("sbuf", [128, 4 * NR], "int32"),
    "hi4": ("sbuf", [128, 4 * NR], "int32"),
    "lo4": ("sbuf", [128, 4 * NR], "int32"),
    "lof": ("sbuf", [128, 4 * NR], "float32"),
    "own": ("sbuf", [128, 4 * NR], "bfloat16"),
    "e4": ("sbuf", [128, 4 * NR], "float32"),
    "w4": ("sbuf", [128, 4 * NR], "bfloat16"),
    "kc": ("sbuf", [128, 4 * NR], "float32"),
    "gs": ("sbuf", [128, 128], "bfloat16"),
    "g2": ("sbuf", [128, 128], "bfloat16"),
    "ones": ("sbuf", [128, NR * OC], "bfloat16"),
    "o256": ("sbuf", [128, 128], "bfloat16"),
    "rep": ("sbuf", [128, NR * OC], "bfloat16"),
    "rep16": ("sbuf", [128, B * 16], "bfloat16"),
    "jj": ("sbuf", [128, NR * OC // 2], "bfloat16"),
    "lst": ("sbuf", [128, 16], "bfloat16"),
    "mst": ("sbuf", [128, 16], "bfloat16"),
    "pidx": ("sbuf", [128, 4], "int32"),
    "pand": ("sbuf", [128, 4], "int32"),
    "pm16": ("sbuf", [128, 4], "float32"),
    "i12": ("sbuf", [128, NR], "float32"),
    "i12b": ("sbuf", [128, NR], "float32"),
    "hif": ("sbuf", [128, 4], "float32"),
    "hh": ("sbuf", [128, NR], "bfloat16"),
    "hhf": ("sbuf", [128, NR], "float32"),
    "tmp": ("sbuf", [128, NR], "float32"),
    "prod": ("sbuf", [128, NR], "float32"),
    "slot": ("sbuf", [128, 4], "float32"),
    "p_code": ("psum", [128, 512], "float32"),
    "p_g": ("psum", [128, 512], "float32"),
    "p_o0": ("psum", [128, 512], "float32"),
    "p_o1": ("psum", [128, 512], "float32"),
    "p_c": ("psum", [128, 512], "float32"),
    "p_r": ("psum", [128, 512], "float32"),
}
SEMAPHORES = ["ld_a", "ld_c", "arr", "sent", "st"] + ["h%d" % i for i in range(8)] + ["q%d" % i for i in range(64)]

_CACHE = {}


def make_plan(cores, topo):
    key = tuple(cores)
    if key in _CACHE:
        return _CACHE[key]
    n = len(cores)
    every = range(topo.CHIPS * topo.CORES_PER_CHIP)
    chips = sorted({topo.chip(c) for c in cores})
    on = {X: [r for r in range(n) if topo.chip(cores[r]) == X] for X in chips}
    mate = {X: [m for m in range(topo.CHIPS) if topo.mates(X, m)][0] for X in chips}

    def links(X, Y, kind):
        if kind == "S":
            return (("o", X), ("i", Y))
        if kind == "M":
            return (("m", X),)
        if kind == "i":
            return (("m", X), ("o", mate[X]), ("i", Y))
        return (("o", X), ("i", mate[Y]), ("m", mate[Y]))

    kind, cross, base = {}, [], {}
    for X in chips:
        for Y in chips:
            if X == Y:
                continue
            if topo.same_plane(X, Y):
                kind[X, Y] = "S"
            elif topo.mates(X, Y):
                kind[X, Y] = "M"
            else:
                cross.append((X, Y))
                continue
            for l in links(X, Y, kind[X, Y]):
                base[l] = base.get(l, 0) + len(on[Y])
    ncap0 = {X: sum(1 for Y in chips if kind.get((X, Y)) == "M") for X in chips}
    opts = [(links(X, Y, "i"), links(X, Y, "ii"), len(on[Y]), X) for X, Y in cross]
    best = None
    for code in range(1 << len(cross)):
        load, ncap = dict(base), dict(ncap0)
        for j, (li, lii, w, X) in enumerate(opts):
            two = code >> j & 1
            if not two:
                ncap[X] += 1
            for l in (lii if two else li):
                load[l] = load.get(l, 0) + w
        if max(ncap.values()) > 2:
            continue
        score = (max(load.values()), bin(code).count("1"), sum(v * v for v in load.values()))
        if best is None or score < best[0]:
            best = (score, code)
    for j, f in enumerate(cross):
        kind[f] = "ii" if best[1] >> j & 1 else "i"

    fw, used, rounds, calls = {}, {}, {}, []

    def hop(src_cols, to, npk, rnd):
        a = used.get(to, 0)
        used[to] = a + npk
        jobs = fw.setdefault(to, [])
        tr = {"src": src_cols, "to": to, "buf": "pk", "dst": (a * PK, (a + npk) * PK), "sem": "h%d" % len(jobs)}
        job = {"sem": tr["sem"], "inc": tr, "trs": [], "rnd": rnd, "cols": tr["dst"]}
        jobs.append(job)
        calls.append((to, job["trs"]))
        return tr, job

    def land(s, r, src_cols):
        i = s if s < r else s - 1
        return {"src": src_cols, "to": cores[r], "buf": "big", "dst": (CW + i * PK, CW + (i + 1) * PK), "sem": "arr",
                "rank": r}

    for s in range(n):
        cs = cores[s]
        X, d = topo.chip(cs), topo.die(cs)
        helpers = [c for c in every if topo.chip(c) == X and topo.die(c) == d and c not in cores]
        i0 = chips.index(X)
        dests = [chips[(i0 + 1 + t) % len(chips)] for t in range(len(chips) - 1)]
        dests.sort(key=lambda Y: 0 if kind[X, Y] == "ii" else 1)
        cap = [Y for Y in dests if kind[X, Y] in ("M", "i")]
        hc = [h for h in helpers if all(topo.may_write(h, cores[r]) for Y in cap for r in on[Y])][0]
        order = [hc] + [h for h in helpers if h != hc]
        hload = {h: 0 for h in order}
        hload[hc] = sum(len(on[Y]) for Y in cap)
        free = [Y for Y in dests if Y not in cap]
        who = {Y: [hc] for Y in cap}
        for Y in free[:-1]:
            h = min(order, key=lambda c: hload[c])
            who[Y] = [h]
            hload[h] += len(on[Y])
        who[free[-1]] = sorted(order, key=lambda c: hload[c])[:len(on[free[-1]])]
        rs = []
        for rnd, Y in enumerate(dests):
            base_col = 2 * rnd * PK
            groups = [on[Y]] if len(who[Y]) == 1 else [[r] for r in on[Y]]
            trs, col = [], base_col
            for gi, dl in enumerate(groups):
                tr, job = hop((col, col + len(dl) * PK), who[Y][gi], len(dl), rnd)
                trs.append(tr)
                col += len(dl) * PK
                if kind[X, Y] == "ii":
                    cands = [c for c in every if topo.chip(c) == mate[Y] and topo.die(c) == d and c not in cores
                             and all(topo.may_write(c, cores[r]) for r in on[Y])]
                    rel = min(cands, key=lambda c: used.get(c, 0))
                    tr2, job2 = hop(job["cols"], rel, len(dl), rnd)
                    job["trs"].append(tr2)
                    job = job2
                for t, r in enumerate(dl):
                    a = job["cols"][0] + t * PK
                    job["trs"].append(land(s, r, (a, a + PK)))
            rs.append({"dst": list(on[Y]), "trs": trs})
            calls.append((cs, trs))
        mine = [r for r in on[X] if r != s]
        for t, r in enumerate(mine):
            a = (2 * len(dests) + t) * PK
            trs = [land(s, r, (a, a + PK))]
            rs.append({"dst": [r], "trs": trs})
            calls.append((cs, trs))
        rounds[s] = rs

    arr = [0] * n
    for src, trs in calls:
        m = -1
        for t in trs:
            m &= topo.mask(src, t["to"])
        bits = [e for e in range(m.bit_length()) if m >> e & 1]
        k = len(bits) // len(trs)
        for i, t in enumerate(trs):
            t["mask"] = sum(1 << e for e in bits[i * k:(i + 1) * k])
            t["ne"] = k
            if "rank" in t:
                arr[t["rank"]] += k
    for c in fw:
        fw[c].sort(key=lambda j: j["rnd"])
    _CACHE[key] = (rounds, fw, arr, kind)
    return _CACHE[key]


def send(g, T, topo, trs):
    lst = []
    for t in trs:
        rid, pid, _se = topo.addr(t["to"])
        lst.append(RemoteDMATransfer(dst_ids=[DstId(rid=rid, pnc=pid)], dma_engine_mask=t["mask"],
                                     remote_sem=T.sem[t["sem"]], src=T.pk[:, t["src"][0]:t["src"][1]],
                                     dst=T[t["buf"]][:, t["dst"][0]:t["dst"][1]]))
    g.remote_dma_fused(lst, local_sem=T.sem.sent)
    return sum(t["ne"] for t in trs)


def rank_program(g, core, T, topo):
    rounds, fw, arr, _kind = make_plan(list(T.cores), topo)
    rank = T.rank_of(core)
    if rank is None:
        sent = 0
        for job in fw.get(core, []):
            g.wait_ge(T.sem[job["sem"]], job["inc"]["ne"])
            sent += send(g, T, topo, job["trs"])
        if sent:
            g.wait_ge(T.sem.sent, sent)
        return

    V, SC, PE, SY = g.vector, g.scalar, g.tensor, g.sync
    A = AluOpType
    sem = T.sem
    nq = [0]

    def new():
        nq[0] += 1
        return sem["q%d" % (nq[0] - 1)]

    K4 = 4 * NR
    HALF = NR * OC // 2

    for k in range(4):
        (SY if k % 2 == 0 else SC).dma_start(T.a4[0:16, k * NR:(k + 1) * NR], T.parent[:, :]).then_inc(sem.ld_a, 16)
    SY.dma_start(T.big[:, 0:CW], T.c[:, :]).then_inc(sem.ld_c, 16)

    s_ones, s_o256 = new(), new()
    V.memset(T.ones[0:K4, :], 1.0).then_inc(s_ones, 1)
    V.memset(T.o256[0:16, :], 256.0).then_inc(s_o256, 1)
    s_pid, s_kc, s_lst, s_mst, s_rep, s_jj = new(), new(), new(), new(), new(), new()
    g.iota(T.pidx[:, 0:1], [[0, 1]], 0, 1).then_inc(s_pid, 1)
    g.iota(T.kc[0:16, 0:K4], [[1, 4], [0, NR]], -16, 0, allow_small_or_imprecise_dtypes=True).then_inc(s_kc, 1)
    g.wait_ge(s_ones, 1)
    g.affine_select(T.lst[0:16, 0:16], T.ones[0:16, 0:16], [[1, 16]], A.is_gt, 0.0, 0, -1).then_inc(s_lst, 1)
    g.wait_ge(s_lst, 1)
    g.affine_select(T.mst[0:16, 0:16], T.lst[0:16, 0:16], [[1, 16]], A.not_equal, -16.0, 0, -1).then_inc(s_mst, 1)
    g.affine_select(T.rep[0:K4, :], T.ones[0:K4, :], [[-1, NR], [-NR, 4], [0, 16]], A.is_equal, 0.0, 0, 1
                    ).then_inc(s_rep, 1)
    g.iota(T.jj[0:1, :], [[0, HALF // 16], [16, 16]], 0, 0, allow_small_or_imprecise_dtypes=True).then_inc(s_jj, 1)
    s_i12, s_i12b, s_rep16 = new(), new(), new()
    g.iota(T.i12[0:16, :], [[1, NR]], 0, 0, allow_small_or_imprecise_dtypes=True).then_inc(s_i12, 1)
    nb = 0
    if rank > 0:
        g.iota(T.i12b[0:16, 0:rank], [[4, rank]], 16, 0, allow_small_or_imprecise_dtypes=True).then_inc(s_i12b, 1)
        nb += 1
    g.iota(T.i12b[0:16, rank:NR], [[4, NR - rank]], 16 + 4 * (rank - 1), 0, allow_small_or_imprecise_dtypes=True
           ).then_inc(s_i12b, 1)
    nb += 1
    g.affine_select(T.rep16[0:16, :], T.ones[0:16, 0:B * 16], [[-1, 16], [0, 16]], A.is_equal, 0.0, 0, 1
                    ).then_inc(s_rep16, 1)
    s_pand, s_pm = new(), new()
    V.wait_ge(s_pid, 1)
    V.tensor_scalar(T.pand[:, 0:1], T.pidx[:, 0:1], 15, None, A.bitwise_and).then_inc(s_pand, 1)
    V.wait_ge(s_pand, 1)
    V.tensor_copy(T.pm16[:, 0:1], T.pand[:, 0:1]).then_inc(s_pm, 1)

    s_hi, s_lo, s_lof, s_own, s_code, s_e, s_w, s_g, s_gs = (new() for _ in range(9))
    V.wait_ge(sem.ld_a, 64)
    V.tensor_scalar(T.hi4[0:16, :], T.a4[0:16, :], 4, None, A.arith_shift_right).then_inc(s_hi, 1)
    V.tensor_scalar(T.lo4[0:16, :], T.a4[0:16, :], 15, None, A.bitwise_and).then_inc(s_lo, 1)
    V.wait_ge(s_hi, 1)
    V.tensor_scalar(T.own[0:16, :], T.hi4[0:16, :], rank, None, A.is_equal).then_inc(s_own, 1)
    V.wait_ge(s_lo, 1)
    V.tensor_copy(T.lof[0:16, :], T.lo4[0:16, :]).then_inc(s_lof, 1)
    PE.wait_ge(s_own, 1)
    PE.wait_ge(s_mst, 1)
    PE.matmul(T.p_code[0:16, 0:K4], T.mst[0:16, 0:16], T.own[0:16, :], True, True).then_inc(s_code, 1)
    V.wait_ge(s_code, 1)
    V.wait_ge(s_kc, 1)
    V.tensor_tensor(T.e4[0:16, :], T.p_code[0:16, 0:K4], T.kc[0:16, :], A.is_equal).then_inc(s_e, 1)
    V.wait_ge(s_e, 1)
    V.wait_ge(s_lof, 1)
    V.tensor_tensor(T.w4[0:16, :], T.e4[0:16, :], T.lof[0:16, :], A.mult).then_inc(s_w, 1)
    PE.wait_ge(s_w, 1)
    PE.wait_ge(s_o256, 1)
    PE.matmul(T.p_g[0:K4, 0:128], T.w4[0:16, :], T.o256[0:16, :], True, True).then_inc(s_g, 1)
    V.wait_ge(s_g, 1)
    V.tensor_copy(T.gs[0:K4, :], T.p_g[0:K4, 0:128]).then_inc(s_gs, 1)
    PE.wait_ge(s_gs, 1)
    PE.wait_ge(s_rep, 1)
    PE.wait_ge(s_jj, 1)
    s_off = []
    V.wait_ge(s_pm, 1)
    for h, po in enumerate((T.p_o0, T.p_o1)):
        s_po, so = new(), new()
        PE.matmul(po[:, 0:HALF], T.gs[0:K4, :], T.rep[0:K4, h * HALF:(h + 1) * HALF], True, False)
        PE.matmul(po[:, 0:HALF], T.ones[0:1, 0:128], T.jj[0:1, :], False, True).then_inc(s_po, 1)
        V.wait_ge(s_po, 1)
        V.tensor_scalar(T.offs[:, h * HALF:(h + 1) * HALF], po[:, 0:HALF], T.pm16[:, 0:1], None, A.add).then_inc(so, 1)
        s_off.append(so)

    for q in (V, SC):
        q.wait_ge(sem.ld_c, 16)
        for so in s_off:
            q.wait_ge(so, 1)
    cwin = T.big[:, 0:CW]
    sent = 0
    col = 0
    for rd in rounds[rank]:
        sv, ss = new(), new()
        if len(rd["dst"]) == 2:
            parts = [(col, PK, rd["dst"][0] * OC), (col + PK, PK, rd["dst"][1] * OC)]
        else:
            parts = [(col, PK // 2, rd["dst"][0] * OC), (col + PK // 2, PK // 2, rd["dst"][0] * OC + OC // 2)]
        (a, w, o) = parts[0]
        V.tensor_copy(T.pk[:, a:a + w], cwin.indirect(T.offs[:, o:o + w // 16])).then_inc(sv, 1)
        (a, w, o) = parts[1]
        SC.activation(T.pk[:, a:a + w], cwin.indirect(T.offs[:, o:o + w // 16]), ActivationFunctionType.Copy
                      ).then_inc(ss, 1)
        col += len(rd["dst"]) * PK
        g.wait_ge(sv, 1)
        g.wait_ge(ss, 1)
        sent += send(g, T, topo, rd["trs"])

    t = [new() for _ in range(12)]
    V.tensor_copy(T.hif[0:16, 0:1], T.hi4[0:16, rank:rank + 1]).then_inc(t[0], 1)
    V.wait_ge(t[0], 1)
    V.wait_ge(s_i12, 1)
    V.tensor_scalar(T.hh[0:16, :], T.i12[0:16, :], T.hif[0:16, 0:1], None, A.is_equal).then_inc(t[1], 1)
    V.tensor_scalar(T.hhf[0:16, :], T.i12[0:16, :], T.hif[0:16, 0:1], None, A.is_equal).then_inc(t[2], 1)
    PE.wait_ge(t[1], 1)
    PE.matmul(T.p_c[0:16, 0:NR], T.lst[0:16, 0:16], T.hh[0:16, :], True, True).then_inc(t[3], 1)
    V.wait_ge(t[3], 1)
    V.wait_ge(s_i12b, nb)
    V.tensor_tensor(T.tmp[0:16, :], T.p_c[0:16, 0:NR], T.i12b[0:16, :], A.add).then_inc(t[4], 1)
    V.wait_ge(t[4], 1)
    V.tensor_copy(T.tmp[0:16, rank:rank + 1], T.lof[0:16, rank:rank + 1]).then_inc(t[5], 1)
    V.wait_ge(t[5], 1)
    V.wait_ge(t[2], 1)
    V.tensor_tensor(T.prod[0:16, :], T.hhf[0:16, :], T.tmp[0:16, :], A.mult).then_inc(t[6], 1)
    V.wait_ge(t[6], 1)
    V.tensor_reduce(T.slot[0:16, 0:1], T.prod[0:16, :], AxisListType.X, A.add).then_inc(t[7], 1)
    V.wait_ge(t[7], 1)
    V.tensor_scalar(T.g2[0:16, :], T.o256[0:16, :], T.slot[0:16, 0:1], None, A.mult).then_inc(t[8], 1)
    PE.wait_ge(t[8], 1)
    PE.wait_ge(s_rep16, 1)
    PE.matmul(T.p_r[:, 0:B * 16], T.g2[0:16, :], T.rep16[0:16, :], True, False)
    PE.matmul(T.p_r[:, 0:B * 16], T.ones[0:1, 0:128], T.jj[0:1, 0:B * 16], False, True).then_inc(t[9], 1)
    V.wait_ge(t[9], 1)
    V.tensor_scalar(T.offr[:, :], T.p_r[:, 0:B * 16], T.pm16[:, 0:1], None, A.add).then_inc(t[10], 1)

    V.wait_ge(t[10], 1)
    SC.wait_ge(t[10], 1)
    V.wait_ge(sem.arr, arr[rank])
    SC.wait_ge(sem.arr, arr[rank])
    win = T.big[:, 0:WIN]
    for c in range(4):
        f = new()
        o = win.indirect(T.offr[:, c * OC:(c + 1) * OC])
        if c % 2 == 0:
            V.tensor_copy(T.ysb[:, c * PK:(c + 1) * PK], o).then_inc(f, 1)
        else:
            SC.activation(T.ysb[:, c * PK:(c + 1) * PK], o, ActivationFunctionType.Copy).then_inc(f, 1)
        SY.wait_ge(f, 1)
        SY.dma_start(T.y[:, c * PK:(c + 1) * PK], T.ysb[:, c * PK:(c + 1) * PK]).then_inc(sem.st, 16)
    SY.wait_ge(sem.st, 64)
    g.wait_ge(sem.sent, sent)
